import numpy as np
import ml_dtypes


def mxq(x, axis, fmt="e4m3"):
    dtype, down = {"e4m3": (ml_dtypes.float8_e4m3fn, 7), "e5m2": (ml_dtypes.float8_e5m2, 14)}[fmt]
    v = np.moveaxis(np.asarray(x, np.float32).astype(ml_dtypes.bfloat16).astype(np.float64), axis, -1)
    blocks = v.reshape(v.shape[:-1] + (-1, 32))
    amax = np.abs(blocks).max(-1, keepdims=True)
    byte = np.maximum(np.where(amax > 0, np.frexp(amax)[1] - 1 + 127, 0) - down, 1)
    scale = np.exp2(byte - 127.0)
    codes = (blocks / scale).astype(np.float32).astype(dtype).astype(np.float64)
    return np.moveaxis((codes * scale).reshape(v.shape), -1, axis)


WIDE = False


def mx_kscale(k):
    if not WIDE:
        return np.ones(k)
    levels = np.array([30, -30])
    if k % 512:
        return np.exp2(np.random.permutation(np.resize(levels, k // 32))).repeat(32)
    a = np.empty((k // 512, 16))
    for p in range(k // 512):
        a[p, :8] = np.random.permutation(np.resize(levels, 8))
        for g in range(8):
            far = levels[np.abs(levels - a[p, g]) >= 10]
            a[p, g + 8] = far[np.random.randint(len(far))]
    return np.exp2(a.ravel()).repeat(32)


def f64(x):
    return np.asarray(x).astype(np.float64)


def striped(idx):
    return np.tile(np.asarray(idx).reshape(-1, 16).T, (8, 1)).astype(np.uint16)


def unstriped(offs):
    return offs[:16].T.reshape(-1).astype(np.int64)


E2M1 = np.array([0.0, 0.5, 1.0, 1.5, 2.0, 3.0, 4.0, 6.0, -0.0, -0.5, -1.0, -1.5, -2.0, -3.0, -4.0, -6.0])


def pack_weight(w, fmt):
    k, n = w.shape
    w = f64(np.asarray(w, np.float32).astype(ml_dtypes.bfloat16)).reshape(k // 32, 32, n)
    amax = np.abs(w).max(1)
    if fmt in ("e4m3", "e5m2"):
        byte = np.frexp(amax)[1] - 1 + 127 - (7 if fmt == "e4m3" else 14)
    else:
        mant, ex = np.frexp(amax / 6.0)
        byte = np.where(mant > 0.5, ex, ex - 1) + 127
    byte = np.clip(np.where(amax > 0, byte, 1), 1, 254)
    scaled = (w * np.exp2(127.0 - byte)[:, None, :]).reshape(k, n).astype(np.float32)
    by_word = np.ascontiguousarray(scaled.reshape(k // 512, 128, 4, n).transpose(0, 1, 3, 2))
    if fmt in ("e4m3", "e5m2"):
        words = by_word.astype(ml_dtypes.float8_e4m3fn if fmt == "e4m3" else ml_dtypes.float8_e5m2).view(np.uint8)
    else:
        c = by_word.astype(ml_dtypes.float4_e2m1fn).view(np.uint8) & 0xF
        words = (c[..., 0::2] | (c[..., 1::2] << 4)).reshape(k // 512, 128, 2 * n)
    return np.ascontiguousarray(words), np.ascontiguousarray(byte.astype(np.uint8).reshape(k // 512, 16, n))


def unpack_weight(words, scales, fmt):
    g, _, n = scales.shape
    words = np.ascontiguousarray(words).reshape(g, 128, n, -1)
    if fmt in ("e4m3", "e5m2"):
        vals = words.view(ml_dtypes.float8_e4m3fn if fmt == "e4m3" else ml_dtypes.float8_e5m2).astype(np.float64)
    else:
        nib = np.empty((g, 128, n, 4), np.uint8)
        nib[..., 0::2] = words & 0xF
        nib[..., 1::2] = words >> 4
        vals = E2M1[nib]
    vals = vals * np.repeat(np.exp2(scales.astype(np.float64) - 127.0), 8, axis=1)[..., None]
    return vals.transpose(0, 1, 3, 2).reshape(g * 512, n)


K, T, J, I, R, C = 512, 512, 256, 256, 512, 512


def setup_inputs():
    n = np.random.standard_normal
    idx = np.random.permutation(T)[:J]
    idx2 = np.random.permutation(C)[:J]
    idx3 = np.random.permutation(T)[:I]
    fk = mx_kscale(K)
    fr = mx_kscale(R)
    xtp = pack_weight(n((K, T)) / fk[:, None], "e5m2")
    wap = pack_weight(n((K, R)) * 0.5 / np.sqrt(K) * fk[:, None] * fr, "e2m1")
    wbp = pack_weight(n((K, R)) * 1 / np.sqrt(K) * fk[:, None] / fr, "e2m1")
    return {
        "xt_words": xtp[0],
        "xt_scales": xtp[1],
        "wa_words": wap[0],
        "wa_scales": wap[1],
        "tf": (n((R, C))).astype(np.float32),
        "wb_words": wbp[0],
        "wb_scales": wbp[1],
        "offs": striped(idx),
        "offs2": striped(idx2),
        "offs3": striped(idx3),
    }


def reference(xt_words, xt_scales, wa_words, wa_scales, tf, wb_words, wb_scales, offs, offs2, offs3):
    idx = unstriped(offs)
    idx2 = unstriped(offs2)
    idx3 = unstriped(offs3)
    xtu = unpack_weight(xt_words, xt_scales, "e5m2")
    wau = unpack_weight(wa_words, wa_scales, "e2m1")
    wbu = unpack_weight(wb_words, wb_scales, "e2m1")
    xtidxg = xtu[:, idx]
    za = wau.T @ xtidxg
    ha = za * f64(tf)[:, idx2]
    xtidx3g = xtu[:, idx3]
    zb = wbu.T @ xtidx3g
    yb1 = np.pad(zb, ((0, 0), (1, 0)))[:, :I]
    hb = zb - 0.6 * yb1
    haq = mxq(ha, 0, "e5m2")
    hbq = mxq(hb, 0, "e5m2")
    a0 = haq.T @ hbq
    mn = np.mean(a0, axis=1, keepdims=True)
    y = 0.04 * np.maximum(a0 - mn, 0.0)
    return y

@@ -1,0 +1,160 @@
+from contextlib import ExitStack
+
+import concourse.mybir as mybir
+
+K, T, J, I, R, C = 512, 512, 256, 256, 512, 512
+FLOPS = 2 * K * R * J + 2 * K * R * I + 2 * R * J * I
+
+F32 = mybir.dt.float32
+BF16 = mybir.dt.bfloat16
+I32 = mybir.dt.int32
+U32 = mybir.dt.uint32
+U16 = mybir.dt.uint16
+U8 = mybir.dt.uint8
+E5M2X4 = mybir.dt.float8_e5m2_x4
+E2M1X4 = mybir.dt.float4_e2m1fn_x4
+ALU = mybir.AluOpType
+ACT = mybir.ActivationFunctionType
+
+P = 128
+PACK = 4
+HALF = 128
+LAG = 0.6
+GAIN = 0.04
+
+
+def tile_list_meet_timestable_lagged_abovemean_kernel(
+    tc, xt_words, xt_scales, wa_words, wa_scales, tf, wb_words, wb_scales, offs, offs2, offs3, out
+):
+    nc = tc.nc
+    with ExitStack() as ctx:
+        sb = ctx.enter_context(tc.tile_pool(name="sb", bufs=1))
+        ps = ctx.enter_context(tc.psum_pool(name="ps", bufs=1))
+
+        list_a = sb.tile([P, J // 16], U16, name="list_a")
+        list_f = sb.tile([P, J // 16], U16, name="list_f")
+        list_b = sb.tile([P, I // 16], U16, name="list_b")
+        x_words = sb.tile([P, T], U32, name="x_words", align_bytes=64)
+        x_scales = sb.tile([P, T], U8, name="x_scales", align_bytes=64)
+        w_raw = {s: sb.tile([P, R // 2], I32, name="w_raw_" + s, align_bytes=64) for s in "ab"}
+        ws_raw = {s: sb.tile([P, R // 4], I32, name="ws_raw_" + s, align_bytes=64) for s in "ab"}
+        w_words = {s: sb.tile([P, 2 * R], U8, name="w_words_" + s, align_bytes=64) for s in "ab"}
+        w_scales = {s: sb.tile([P, R], U8, name="w_scales_" + s, align_bytes=64) for s in "ab"}
+        table = [sb.tile([P, C], F32, name="table%d" % t, align_bytes=64) for t in range(PACK)]
+
+        def load_scale_rows(queue, plane, rows):
+            for q in range(4):
+                queue.dma_start(out=plane[32 * q : 32 * q + 4, :], in_=rows[0, 4 * q : 4 * q + 4, :].bitcast(I32))
+
+        nc.vector.memset(x_scales[:].bitcast(I32), 0)
+        nc.vector.memset(ws_raw["b"][:], 0)
+        nc.vector.memset(ws_raw["a"][:], 0)
+
+        tf_rows = tf.rearrange("(g t e) c -> t g e c", t=PACK, e=8)
+        nc.gpsimd.dma_start(out=w_raw["a"][:], in_=wa_words[0].bitcast(I32))
+        nc.gpsimd.dma_start(out=table[3][:], in_=tf_rows[3])
+        nc.sync.dma_start(out=list_b[:], in_=offs3)
+        nc.sync.dma_start(out=x_words[:].bitcast(I32), in_=xt_words[0].rearrange("p n t -> p (n t)").bitcast(I32))
+        load_scale_rows(nc.sync, x_scales[:].bitcast(I32), xt_scales)
+        nc.sync.dma_start(out=w_raw["b"][:], in_=wb_words[0].bitcast(I32))
+        nc.sync.dma_start(out=list_a[:], in_=offs)
+        load_scale_rows(nc.sync, ws_raw["b"], wb_scales)
+        nc.sync.dma_start(out=list_f[:], in_=offs2)
+        for t in range(3):
+            nc.sync.dma_start(out=table[t][:], in_=tf_rows[t])
+        load_scale_rows(nc.sync, ws_raw["a"], wa_scales)
+
+        def deal_weight(s):
+            nc.gpsimd.tensor_copy(
+                out=w_words[s][:].bitcast(I32).rearrange("p (t g w) -> p t g w", t=PACK, w=4),
+                in_=w_raw[s][:].rearrange("p (g t w) -> p t g w", t=PACK, w=4),
+            )
+            eng = nc.vector if s == "b" else nc.gpsimd
+            eng.tensor_copy(
+                out=w_scales[s][:].bitcast(I32).rearrange("p (t g w) -> p t g w", t=PACK, w=2),
+                in_=ws_raw[s][:].rearrange("p (g t w) -> p t g w", t=PACK, w=2),
+            )
+
+        def first_product(s, offsets, h):
+            cols = offsets[:, 8 * h : 8 * h + 8]
+            words = sb.tile([P, HALF], U32, name="g_words_%s%d" % (s, h), align_bytes=64)
+            scales = sb.tile([P, HALF], U8, name="g_scales_%s%d" % (s, h), align_bytes=64)
+            nc.vector.tensor_copy(out=words[:], in_=x_words[:].indirect(cols))
+            nc.vector.tensor_copy(out=scales[:], in_=x_scales[:].indirect(cols))
+            z = ps.tile([P, PACK, HALF], F32, name="z_%s%d" % (s, h))
+            for t in range(PACK):
+                nc.tensor.matmul_mx(
+                    out=z[:, t, :],
+                    lhsT=w_words[s][:, 2 * P * t : 2 * P * (t + 1)].bitcast(E2M1X4),
+                    lhsT_scale=w_scales[s][:, P * t : P * (t + 1)],
+                    rhs=words[:].bitcast(E5M2X4),
+                    rhs_scale=scales[:],
+                    start=True,
+                    stop=True,
+                )
+            return z
+
+        deal_weight("b")
+        zb = [first_product("b", list_b, h) for h in range(2)]
+        deal_weight("a")
+        za = [first_product("a", list_a, h) for h in range(2)]
+
+        zb_sb = sb.tile([P, PACK * (I + 1)], F32, name="zb_sb", align_bytes=64)
+        nc.vector.memset(zb_sb[:, 0:PACK], 0.0)
+        hb = sb.tile([P, PACK * I], BF16, name="hb", align_bytes=64)
+        W = PACK * HALF
+        for h in range(2):
+            nc.scalar.activation(
+                out=zb_sb[:, PACK + W * h : PACK + W * (h + 1)].rearrange("p (i t) -> p i t", t=PACK),
+                in_=zb[h][:].rearrange("p t i -> p i t"),
+                func=ACT.Copy,
+            )
+        for h in range(2):
+            nc.vector.scalar_tensor_tensor(
+                out=hb[:, W * h : W * (h + 1)],
+                in0=zb_sb[:, W * h : W * (h + 1)],
+                scalar=-LAG,
+                in1=zb_sb[:, PACK + W * h : PACK + W * (h + 1)],
+                op0=ALU.mult,
+                op1=ALU.add,
+            )
+        hb_codes = sb.tile([P, I], U32, name="hb_codes", align_bytes=64)
+        hb_scales = sb.tile([P, I], U8, name="hb_scales", align_bytes=64)
+        nc.vector.quantize_mx(out=hb_codes[:].bitcast(E5M2X4), scales=hb_scales[:], in_=hb[:])
+
+        factors = sb.tile([P, PACK, J], F32, name="factors", align_bytes=64)
+        for t in range(PACK):
+            if t == 1:
+                nc.vector.tensor_copy(out=factors[:, t, :], in_=table[t][:].indirect(list_f[:]))
+            else:
+                nc.scalar.activation(out=factors[:, t, :], in_=table[t][:].indirect(list_f[:]), func=ACT.Copy)
+
+        for h in range(2):
+            ha = sb.tile([P, W], BF16, name="ha%d" % h, align_bytes=64)
+            nc.vector.tensor_tensor(
+                out=ha[:].rearrange("p (c j t) -> p c t j", j=4, t=PACK),
+                in0=za[h][:].rearrange("p t (c j) -> p c t j", j=4),
+                in1=factors[:, :, HALF * h : HALF * (h + 1)].rearrange("p t (c j) -> p c t j", j=4),
+                op=ALU.mult,
+            )
+            ha_codes = sb.tile([P, HALF], U32, name="ha_codes%d" % h, align_bytes=64)
+            ha_scales = sb.tile([P, HALF], U8, name="ha_scales%d" % h, align_bytes=64)
+            nc.vector.quantize_mx(out=ha_codes[:].bitcast(E5M2X4), scales=ha_scales[:], in_=ha[:])
+            a0 = ps.tile([P, I], F32, name="a0_%d" % h)
+            nc.tensor.matmul_mx(
+                out=a0[:],
+                lhsT=ha_codes[:].bitcast(E5M2X4),
+                lhsT_scale=ha_scales[:],
+                rhs=hb_codes[:].bitcast(E5M2X4),
+                rhs_scale=hb_scales[:],
+                start=True,
+                stop=True,
+            )
+            shares = sb.tile([P, I], F32, name="shares%d" % h, align_bytes=64)
+            bias = sb.tile([P, 1], F32, name="bias%d" % h)
+            nc.vector.tensor_scalar(
+                out=shares[:], in0=a0[:], scalar1=-GAIN / I, scalar2=None, op0=ALU.mult, op1=ALU.add, accum_out=bias[:]
+            )
+            y = sb.tile([P, I], F32, name="y%d" % h, align_bytes=64)
+            nc.scalar.activation(out=y[:], in_=shares[:], func=ACT.Relu, bias=bias[:], scale=-float(I))
+            nc.sync.dma_start(out=out[HALF * h : HALF * (h + 1), :], in_=y[:])

@@ -47,33 +47,41 @@ def tile_list_meet_timestable_lagged_abovemean_kernel(
                 queue.dma_start(out=plane[32 * q : 32 * q + 4, :], in_=rows[0, 4 * q : 4 * q + 4, :].bitcast(I32))
 
         nc.vector.memset(x_scales[:].bitcast(I32), 0)
-        nc.vector.memset(ws_raw["b"][:], 0)
+        zeros = sb.tile([P, PACK], F32, name="zeros")
+        nc.vector.memset(w_scales["b"][:].bitcast(I32), 0)
+        nc.vector.memset(zeros[:], 0.0)
         nc.vector.memset(ws_raw["a"][:], 0)
 
         tf_rows = tf.rearrange("(g t e) c -> t g e c", t=PACK, e=8)
-        nc.gpsimd.dma_start(out=w_raw["a"][:], in_=wa_words[0].bitcast(I32))
-        nc.gpsimd.dma_start(out=table[3][:], in_=tf_rows[3])
+        for t in (3, 2):
+            nc.gpsimd.dma_start(out=table[t][:], in_=tf_rows[t])
         nc.sync.dma_start(out=list_b[:], in_=offs3)
-        nc.sync.dma_start(out=x_words[:].bitcast(I32), in_=xt_words[0].rearrange("p n t -> p (n t)").bitcast(I32))
-        load_scale_rows(nc.sync, x_scales[:].bitcast(I32), xt_scales)
-        nc.sync.dma_start(out=w_raw["b"][:], in_=wb_words[0].bitcast(I32))
-        nc.sync.dma_start(out=list_a[:], in_=offs)
         load_scale_rows(nc.sync, ws_raw["b"], wb_scales)
+        nc.sync.dma_start(out=x_words[:].bitcast(I32), in_=xt_words[0].rearrange("p n t -> p (n t)").bitcast(I32))
+        nc.sync.dma_start(out=w_raw["b"][:], in_=wb_words[0].bitcast(I32))
         nc.sync.dma_start(out=list_f[:], in_=offs2)
-        for t in range(3):
-            nc.sync.dma_start(out=table[t][:], in_=tf_rows[t])
+        load_scale_rows(nc.sync, x_scales[:].bitcast(I32), xt_scales)
+        nc.sync.dma_start(out=list_a[:], in_=offs)
+        nc.sync.dma_start(out=w_raw["a"][:], in_=wa_words[0].bitcast(I32))
+        nc.sync.dma_start(out=table[1][:], in_=tf_rows[1])
         load_scale_rows(nc.sync, ws_raw["a"], wa_scales)
+        nc.sync.dma_start(out=table[0][:], in_=tf_rows[0])
+
+        def deal(eng, dst, src, w):
+            eng.tensor_copy(
+                out=dst.bitcast(I32).rearrange("p (t g w) -> p t g w", t=PACK, w=w),
+                in_=src.rearrange("p (g t w) -> p t g w", t=PACK, w=w),
+            )
 
         def deal_weight(s):
-            nc.gpsimd.tensor_copy(
-                out=w_words[s][:].bitcast(I32).rearrange("p (t g w) -> p t g w", t=PACK, w=4),
-                in_=w_raw[s][:].rearrange("p (g t w) -> p t g w", t=PACK, w=4),
-            )
-            eng = nc.vector if s == "b" else nc.gpsimd
-            eng.tensor_copy(
-                out=w_scales[s][:].bitcast(I32).rearrange("p (t g w) -> p t g w", t=PACK, w=2),
-                in_=ws_raw[s][:].rearrange("p (g t w) -> p t g w", t=PACK, w=2),
-            )
+            if s == "b":
+                for q in range(4):
+                    rows = slice(32 * q, 32 * q + 4)
+                    deal(nc.vector, w_scales[s][rows, :], ws_raw[s][rows, :], 2)
+                deal(nc.vector, w_words[s][:], w_raw[s][:], 4)
+            else:
+                deal(nc.gpsimd, w_words[s][:], w_raw[s][:], 4)
+                deal(nc.gpsimd, w_scales[s][:], ws_raw[s][:], 2)
 
         def first_product(s, offsets, h):
             cols = offsets[:, 8 * h : 8 * h + 8]
@@ -99,42 +107,47 @@ def tile_list_meet_timestable_lagged_abovemean_kernel(
         deal_weight("a")
         za = [first_product("a", list_a, h) for h in range(2)]
 
-        zb_sb = sb.tile([P, PACK * (I + 1)], F32, name="zb_sb", align_bytes=64)
-        nc.vector.memset(zb_sb[:, 0:PACK], 0.0)
-        hb = sb.tile([P, PACK * I], BF16, name="hb", align_bytes=64)
+        lagged = sb.tile([P, PACK * I], F32, name="lagged", align_bytes=64)
+        nc.scalar.activation(out=lagged[:, 0:PACK], in_=zeros[:], func=ACT.Copy)
         W = PACK * HALF
         for h in range(2):
+            n = min(HALF, I - 1 - HALF * h)
             nc.scalar.activation(
-                out=zb_sb[:, PACK + W * h : PACK + W * (h + 1)].rearrange("p (i t) -> p i t", t=PACK),
-                in_=zb[h][:].rearrange("p t i -> p i t"),
+                out=lagged[:, PACK + W * h : PACK + W * h + PACK * n].rearrange("p (i t) -> p i t", t=PACK),
+                in_=zb[h][:, :, 0:n].rearrange("p t i -> p i t"),
                 func=ACT.Copy,
-            )
-        for h in range(2):
-            nc.vector.scalar_tensor_tensor(
-                out=hb[:, W * h : W * (h + 1)],
-                in0=zb_sb[:, W * h : W * (h + 1)],
-                scalar=-LAG,
-                in1=zb_sb[:, PACK + W * h : PACK + W * (h + 1)],
-                op0=ALU.mult,
-                op1=ALU.add,
             )
         hb_codes = sb.tile([P, I], U32, name="hb_codes", align_bytes=64)
         hb_scales = sb.tile([P, I], U8, name="hb_scales", align_bytes=64)
-        nc.vector.quantize_mx(out=hb_codes[:].bitcast(E5M2X4), scales=hb_scales[:], in_=hb[:])
+        for h in range(2):
+            hb = sb.tile([P, W], BF16, name="hb%d" % h, tag="rounded", bufs=2, align_bytes=64)
+            nc.vector.scalar_tensor_tensor(
+                out=hb[:].rearrange("p (i t) -> p i t", t=PACK),
+                in0=lagged[:, W * h : W * (h + 1)].rearrange("p (i t) -> p i t", t=PACK),
+                scalar=-LAG,
+                in1=zb[h][:].rearrange("p t i -> p i t"),
+                op0=ALU.mult,
+                op1=ALU.add,
+            )
+            cols = slice(HALF * h, HALF * (h + 1))
+            nc.vector.quantize_mx(out=hb_codes[:, cols].bitcast(E5M2X4), scales=hb_scales[:, cols], in_=hb[:])
 
-        factors = sb.tile([P, PACK, J], F32, name="factors", align_bytes=64)
-        for t in range(PACK):
-            if t == 1:
-                nc.vector.tensor_copy(out=factors[:, t, :], in_=table[t][:].indirect(list_f[:]))
-            else:
-                nc.scalar.activation(out=factors[:, t, :], in_=table[t][:].indirect(list_f[:]), func=ACT.Copy)
+        factors = [sb.tile([P, PACK, HALF], F32, name="factors%d" % h, align_bytes=64) for h in range(2)]
+        for slices in ((3, 2), (1, 0)):
+            for h in range(2):
+                for t in slices:
+                    picked = table[t][:].indirect(list_f[:, 8 * h : 8 * h + 8])
+                    if (t, h) == (1, 0):
+                        nc.vector.tensor_copy(out=factors[h][:, t, :], in_=picked)
+                    else:
+                        nc.scalar.activation(out=factors[h][:, t, :], in_=picked, func=ACT.Copy)
 
         for h in range(2):
-            ha = sb.tile([P, W], BF16, name="ha%d" % h, align_bytes=64)
+            ha = sb.tile([P, W], BF16, name="ha%d" % h, tag="rounded", bufs=2, align_bytes=64)
             nc.vector.tensor_tensor(
                 out=ha[:].rearrange("p (c j t) -> p c t j", j=4, t=PACK),
                 in0=za[h][:].rearrange("p t (c j) -> p c t j", j=4),
-                in1=factors[:, :, HALF * h : HALF * (h + 1)].rearrange("p t (c j) -> p c t j", j=4),
+                in1=factors[h][:].rearrange("p t (c j) -> p c t j", j=4),
                 op=ALU.mult,
             )
             ha_codes = sb.tile([P, HALF], U32, name="ha_codes%d" % h, align_bytes=64)
@@ -152,9 +165,12 @@ def tile_list_meet_timestable_lagged_abovemean_kernel(
             )
             shares = sb.tile([P, I], F32, name="shares%d" % h, align_bytes=64)
             bias = sb.tile([P, 1], F32, name="bias%d" % h)
-            nc.vector.tensor_scalar(
-                out=shares[:], in0=a0[:], scalar1=-GAIN / I, scalar2=None, op0=ALU.mult, op1=ALU.add, accum_out=bias[:]
-            )
+            if h == 0:
+                nc.scalar.activation(out=shares[:], in_=a0[:], func=ACT.Copy, scale=-GAIN / I, accum_out=bias[:])
+            else:
+                nc.vector.tensor_scalar(
+                    out=shares[:], in0=a0[:], scalar1=-GAIN / I, scalar2=None, op0=ALU.mult, op1=ALU.add, accum_out=bias[:]
+                )
             y = sb.tile([P, I], F32, name="y%d" % h, align_bytes=64)
             nc.scalar.activation(out=y[:], in_=shares[:], func=ACT.Relu, bias=bias[:], scale=-float(I))
             nc.sync.dma_start(out=out[HALF * h : HALF * (h + 1), :], in_=y[:])

@@ -42,8 +42,8 @@ def tile_list_meet_timestable_lagged_abovemean_kernel(
         w_scales = {s: sb.tile([P, R], U8, name="w_scales_" + s, align_bytes=64) for s in "ab"}
         table = [sb.tile([P, C], F32, name="table%d" % t, align_bytes=64) for t in range(PACK)]
 
-        def load_scale_rows(queue, plane, rows):
-            for q in range(4):
+        def load_scale_rows(queue, plane, rows, quadrants):
+            for q in quadrants:
                 queue.dma_start(out=plane[32 * q : 32 * q + 4, :], in_=rows[0, 4 * q : 4 * q + 4, :].bitcast(I32))
 
         nc.vector.memset(x_scales[:].bitcast(I32), 0)
@@ -56,16 +56,17 @@ def tile_list_meet_timestable_lagged_abovemean_kernel(
         for t in (3, 2):
             nc.gpsimd.dma_start(out=table[t][:], in_=tf_rows[t])
         nc.sync.dma_start(out=list_b[:], in_=offs3)
-        load_scale_rows(nc.sync, ws_raw["b"], wb_scales)
-        nc.sync.dma_start(out=x_words[:].bitcast(I32), in_=xt_words[0].rearrange("p n t -> p (n t)").bitcast(I32))
-        nc.sync.dma_start(out=w_raw["b"][:], in_=wb_words[0].bitcast(I32))
         nc.sync.dma_start(out=list_f[:], in_=offs2)
-        load_scale_rows(nc.sync, x_scales[:].bitcast(I32), xt_scales)
+        load_scale_rows(nc.scalar, ws_raw["b"], wb_scales, (0, 1))
+        nc.sync.dma_start(out=x_words[:].bitcast(I32), in_=xt_words[0].rearrange("p n t -> p (n t)").bitcast(I32))
+        load_scale_rows(nc.scalar, ws_raw["b"], wb_scales, (2, 3))
+        nc.sync.dma_start(out=w_raw["b"][:], in_=wb_words[0].bitcast(I32))
+        load_scale_rows(nc.sync, x_scales[:].bitcast(I32), xt_scales, range(4))
         nc.sync.dma_start(out=list_a[:], in_=offs)
         nc.sync.dma_start(out=w_raw["a"][:], in_=wa_words[0].bitcast(I32))
-        nc.sync.dma_start(out=table[1][:], in_=tf_rows[1])
-        load_scale_rows(nc.sync, ws_raw["a"], wa_scales)
-        nc.sync.dma_start(out=table[0][:], in_=tf_rows[0])
+        load_scale_rows(nc.sync, ws_raw["a"], wa_scales, range(4))
+        for t in (1, 0):
+            nc.sync.dma_start(out=table[t][:], in_=tf_rows[t])
 
         def deal(eng, dst, src, w):
             eng.tensor_copy(
@@ -107,49 +108,49 @@ def tile_list_meet_timestable_lagged_abovemean_kernel(
         deal_weight("a")
         za = [first_product("a", list_a, h) for h in range(2)]
 
-        lagged = sb.tile([P, PACK * I], F32, name="lagged", align_bytes=64)
+        lagged = sb.tile([P, PACK * (I + 1)], F32, name="lagged", align_bytes=64)
         nc.scalar.activation(out=lagged[:, 0:PACK], in_=zeros[:], func=ACT.Copy)
         W = PACK * HALF
-        for h in range(2):
-            n = min(HALF, I - 1 - HALF * h)
-            nc.scalar.activation(
-                out=lagged[:, PACK + W * h : PACK + W * h + PACK * n].rearrange("p (i t) -> p i t", t=PACK),
-                in_=zb[h][:, :, 0:n].rearrange("p t i -> p i t"),
-                func=ACT.Copy,
-            )
+        STEP = HALF // 2
         hb_codes = sb.tile([P, I], U32, name="hb_codes", align_bytes=64)
         hb_scales = sb.tile([P, I], U8, name="hb_scales", align_bytes=64)
         for h in range(2):
             hb = sb.tile([P, W], BF16, name="hb%d" % h, tag="rounded", bufs=2, align_bytes=64)
-            nc.vector.scalar_tensor_tensor(
-                out=hb[:].rearrange("p (i t) -> p i t", t=PACK),
-                in0=lagged[:, W * h : W * (h + 1)].rearrange("p (i t) -> p i t", t=PACK),
-                scalar=-LAG,
-                in1=zb[h][:].rearrange("p t i -> p i t"),
-                op0=ALU.mult,
-                op1=ALU.add,
-            )
+            for lo in range(0, HALF, STEP):
+                i0 = HALF * h + lo
+                nc.scalar.activation(
+                    out=lagged[:, PACK * (i0 + 1) : PACK * (i0 + 1 + STEP)].rearrange("p (i t) -> p i t", t=PACK),
+                    in_=zb[h][:, :, lo : lo + STEP].rearrange("p t i -> p i t"),
+                    func=ACT.Copy,
+                )
+                nc.vector.scalar_tensor_tensor(
+                    out=hb[:, PACK * lo : PACK * (lo + STEP)],
+                    in0=lagged[:, PACK * i0 : PACK * (i0 + STEP)],
+                    scalar=-LAG,
+                    in1=lagged[:, PACK * (i0 + 1) : PACK * (i0 + 1 + STEP)],
+                    op0=ALU.mult,
+                    op1=ALU.add,
+                )
             cols = slice(HALF * h, HALF * (h + 1))
             nc.vector.quantize_mx(out=hb_codes[:, cols].bitcast(E5M2X4), scales=hb_scales[:, cols], in_=hb[:])
 
         factors = [sb.tile([P, PACK, HALF], F32, name="factors%d" % h, align_bytes=64) for h in range(2)]
-        for slices in ((3, 2), (1, 0)):
-            for h in range(2):
-                for t in slices:
-                    picked = table[t][:].indirect(list_f[:, 8 * h : 8 * h + 8])
-                    if (t, h) == (1, 0):
-                        nc.vector.tensor_copy(out=factors[h][:, t, :], in_=picked)
-                    else:
-                        nc.scalar.activation(out=factors[h][:, t, :], in_=picked, func=ACT.Copy)
+        for t, h in ((3, 0), (3, 1), (2, 0), (2, 1), (1, 0), (0, 0), (1, 1), (0, 1)):
+            picked = table[t][:].indirect(list_f[:, 8 * h : 8 * h + 8])
+            nc.scalar.activation(out=factors[h][:, t, :], in_=picked, func=ACT.Copy)
 
+        rounded_a = []
         for h in range(2):
             ha = sb.tile([P, W], BF16, name="ha%d" % h, tag="rounded", bufs=2, align_bytes=64)
             nc.vector.tensor_tensor(
-                out=ha[:].rearrange("p (c j t) -> p c t j", j=4, t=PACK),
-                in0=za[h][:].rearrange("p t (c j) -> p c t j", j=4),
-                in1=factors[h][:].rearrange("p t (c j) -> p c t j", j=4),
+                out=ha[:].rearrange("p (j t) -> p j t", t=PACK),
+                in0=za[h][:].rearrange("p t j -> p j t"),
+                in1=factors[h][:].rearrange("p t j -> p j t"),
                 op=ALU.mult,
             )
+            rounded_a.append(ha)
+        for h in range(2):
+            ha = rounded_a[h]
             ha_codes = sb.tile([P, HALF], U32, name="ha_codes%d" % h, align_bytes=64)
             ha_scales = sb.tile([P, HALF], U8, name="ha_scales%d" % h, align_bytes=64)
             nc.vector.quantize_mx(out=ha_codes[:].bitcast(E5M2X4), scales=ha_scales[:], in_=ha[:])

from contextlib import ExitStack

import concourse.mybir as mybir

K, T, J, I, R, C = 512, 512, 256, 256, 512, 512
FLOPS = 2 * K * R * J + 2 * K * R * I + 2 * R * J * I

F32 = mybir.dt.float32
BF16 = mybir.dt.bfloat16
I32 = mybir.dt.int32
U32 = mybir.dt.uint32
U16 = mybir.dt.uint16
U8 = mybir.dt.uint8
E5M2X4 = mybir.dt.float8_e5m2_x4
E2M1X4 = mybir.dt.float4_e2m1fn_x4
ALU = mybir.AluOpType
ACT = mybir.ActivationFunctionType

P = 128
PACK = 4
HALF = 128
LAG = 0.6
GAIN = 0.04


def tile_list_meet_timestable_lagged_abovemean_kernel(
    tc, xt_words, xt_scales, wa_words, wa_scales, tf, wb_words, wb_scales, offs, offs2, offs3, out
):
    nc = tc.nc
    with ExitStack() as ctx:
        sb = ctx.enter_context(tc.tile_pool(name="sb", bufs=1))
        ps = ctx.enter_context(tc.psum_pool(name="ps", bufs=1))

        list_a = sb.tile([P, J // 16], U16, name="list_a")
        list_f = sb.tile([P, J // 16], U16, name="list_f")
        list_b = sb.tile([P, I // 16], U16, name="list_b")
        x_words = sb.tile([P, T], U32, name="x_words", align_bytes=64)
        x_scales = sb.tile([P, T], U8, name="x_scales", align_bytes=64)
        w_raw = {s: sb.tile([P, R // 2], I32, name="w_raw_" + s, align_bytes=64) for s in "ab"}
        ws_raw = {s: sb.tile([P, R // 4], I32, name="ws_raw_" + s, align_bytes=64) for s in "ab"}
        w_words = {s: sb.tile([P, 2 * R], U8, name="w_words_" + s, align_bytes=64) for s in "ab"}
        w_scales = {s: sb.tile([P, R], U8, name="w_scales_" + s, align_bytes=64) for s in "ab"}
        table = [sb.tile([P, C], F32, name="table%d" % t, align_bytes=64) for t in range(PACK)]

        def load_scale_rows(queue, plane, rows, quadrants):
            for q in quadrants:
                queue.dma_start(out=plane[32 * q : 32 * q + 4, :], in_=rows[0, 4 * q : 4 * q + 4, :].bitcast(I32))

        nc.vector.memset(x_scales[:].bitcast(I32), 0)
        zeros = sb.tile([P, PACK], F32, name="zeros")
        nc.vector.memset(w_scales["b"][:].bitcast(I32), 0)
        nc.vector.memset(zeros[:], 0.0)
        nc.vector.memset(ws_raw["a"][:], 0)

        tf_rows = tf.rearrange("(g t e) c -> t g e c", t=PACK, e=8)
        for t in (3, 2):
            nc.gpsimd.dma_start(out=table[t][:], in_=tf_rows[t])
        nc.sync.dma_start(out=list_b[:], in_=offs3)
        nc.sync.dma_start(out=list_f[:], in_=offs2)
        load_scale_rows(nc.scalar, ws_raw["b"], wb_scales, (0, 1))
        nc.sync.dma_start(out=x_words[:].bitcast(I32), in_=xt_words[0].rearrange("p n t -> p (n t)").bitcast(I32))
        load_scale_rows(nc.scalar, ws_raw["b"], wb_scales, (2, 3))
        nc.sync.dma_start(out=w_raw["b"][:], in_=wb_words[0].bitcast(I32))
        load_scale_rows(nc.sync, x_scales[:].bitcast(I32), xt_scales, range(4))
        nc.sync.dma_start(out=list_a[:], in_=offs)
        nc.sync.dma_start(out=w_raw["a"][:], in_=wa_words[0].bitcast(I32))
        load_scale_rows(nc.sync, ws_raw["a"], wa_scales, range(4))
        for t in (1, 0):
            nc.sync.dma_start(out=table[t][:], in_=tf_rows[t])

        def deal(eng, dst, src, w):
            eng.tensor_copy(
                out=dst.bitcast(I32).rearrange("p (t g w) -> p t g w", t=PACK, w=w),
                in_=src.rearrange("p (g t w) -> p t g w", t=PACK, w=w),
            )

        def deal_weight(s):
            if s == "b":
                for q in range(4):
                    rows = slice(32 * q, 32 * q + 4)
                    deal(nc.vector, w_scales[s][rows, :], ws_raw[s][rows, :], 2)
                deal(nc.vector, w_words[s][:], w_raw[s][:], 4)
            else:
                deal(nc.gpsimd, w_words[s][:], w_raw[s][:], 4)
                deal(nc.gpsimd, w_scales[s][:], ws_raw[s][:], 2)

        def first_product(s, offsets, h):
            cols = offsets[:, 8 * h : 8 * h + 8]
            words = sb.tile([P, HALF], U32, name="g_words_%s%d" % (s, h), align_bytes=64)
            scales = sb.tile([P, HALF], U8, name="g_scales_%s%d" % (s, h), align_bytes=64)
            nc.vector.tensor_copy(out=words[:], in_=x_words[:].indirect(cols))
            nc.vector.tensor_copy(out=scales[:], in_=x_scales[:].indirect(cols))
            z = ps.tile([P, PACK, HALF], F32, name="z_%s%d" % (s, h))
            for t in range(PACK):
                nc.tensor.matmul_mx(
                    out=z[:, t, :],
                    lhsT=w_words[s][:, 2 * P * t : 2 * P * (t + 1)].bitcast(E2M1X4),
                    lhsT_scale=w_scales[s][:, P * t : P * (t + 1)],
                    rhs=words[:].bitcast(E5M2X4),
                    rhs_scale=scales[:],
                    start=True,
                    stop=True,
                )
            return z

        deal_weight("b")
        zb = [first_product("b", list_b, h) for h in range(2)]
        deal_weight("a")
        za = [first_product("a", list_a, h) for h in range(2)]

        lagged = sb.tile([P, PACK * (I + 1)], F32, name="lagged", align_bytes=64)
        nc.scalar.activation(out=lagged[:, 0:PACK], in_=zeros[:], func=ACT.Copy)
        W = PACK * HALF
        STEP = HALF // 2
        hb_codes = sb.tile([P, I], U32, name="hb_codes", align_bytes=64)
        hb_scales = sb.tile([P, I], U8, name="hb_scales", align_bytes=64)
        for h in range(2):
            hb = sb.tile([P, W], BF16, name="hb%d" % h, tag="rounded", bufs=2, align_bytes=64)
            for lo in range(0, HALF, STEP):
                i0 = HALF * h + lo
                nc.scalar.activation(
                    out=lagged[:, PACK * (i0 + 1) : PACK * (i0 + 1 + STEP)].rearrange("p (i t) -> p i t", t=PACK),
                    in_=zb[h][:, :, lo : lo + STEP].rearrange("p t i -> p i t"),
                    func=ACT.Copy,
                )
                nc.vector.scalar_tensor_tensor(
                    out=hb[:, PACK * lo : PACK * (lo + STEP)],
                    in0=lagged[:, PACK * i0 : PACK * (i0 + STEP)],
                    scalar=-LAG,
                    in1=lagged[:, PACK * (i0 + 1) : PACK * (i0 + 1 + STEP)],
                    op0=ALU.mult,
                    op1=ALU.add,
                )
            cols = slice(HALF * h, HALF * (h + 1))
            nc.vector.quantize_mx(out=hb_codes[:, cols].bitcast(E5M2X4), scales=hb_scales[:, cols], in_=hb[:])

        factors = [sb.tile([P, PACK, HALF], F32, name="factors%d" % h, align_bytes=64) for h in range(2)]
        for t, h in ((3, 0), (3, 1), (2, 0), (2, 1), (1, 0), (0, 0), (1, 1), (0, 1)):
            picked = table[t][:].indirect(list_f[:, 8 * h : 8 * h + 8])
            nc.scalar.activation(out=factors[h][:, t, :], in_=picked, func=ACT.Copy)

        rounded_a = []
        for h in range(2):
            ha = sb.tile([P, W], BF16, name="ha%d" % h, tag="rounded", bufs=2, align_bytes=64)
            nc.vector.tensor_tensor(
                out=ha[:].rearrange("p (j t) -> p j t", t=PACK),
                in0=za[h][:].rearrange("p t j -> p j t"),
                in1=factors[h][:].rearrange("p t j -> p j t"),
                op=ALU.mult,
            )
            rounded_a.append(ha)
        for h in range(2):
            ha = rounded_a[h]
            ha_codes = sb.tile([P, HALF], U32, name="ha_codes%d" % h, align_bytes=64)
            ha_scales = sb.tile([P, HALF], U8, name="ha_scales%d" % h, align_bytes=64)
            nc.vector.quantize_mx(out=ha_codes[:].bitcast(E5M2X4), scales=ha_scales[:], in_=ha[:])
            a0 = ps.tile([P, I], F32, name="a0_%d" % h)
            nc.tensor.matmul_mx(
                out=a0[:],
                lhsT=ha_codes[:].bitcast(E5M2X4),
                lhsT_scale=ha_scales[:],
                rhs=hb_codes[:].bitcast(E5M2X4),
                rhs_scale=hb_scales[:],
                start=True,
                stop=True,
            )
            shares = sb.tile([P, I], F32, name="shares%d" % h, align_bytes=64)
            bias = sb.tile([P, 1], F32, name="bias%d" % h)
            if h == 0:
                nc.scalar.activation(out=shares[:], in_=a0[:], func=ACT.Copy, scale=-GAIN / I, accum_out=bias[:])
            else:
                nc.vector.tensor_scalar(
                    out=shares[:], in0=a0[:], scalar1=-GAIN / I, scalar2=None, op0=ALU.mult, op1=ALU.add, accum_out=bias[:]
                )
            y = sb.tile([P, I], F32, name="y%d" % h, align_bytes=64)
            nc.scalar.activation(out=y[:], in_=shares[:], func=ACT.Relu, bias=bias[:], scale=-float(I))
            nc.sync.dma_start(out=out[HALF * h : HALF * (h + 1), :], in_=y[:])
